import numpy as np
import ml_dtypes


def mxq(x, axis, fmt="e4m3"):
    dtype, down = {"e4m3": (ml_dtypes.float8_e4m3fn, 7), "e5m2": (ml_dtypes.float8_e5m2, 14)}[fmt]
    v = np.moveaxis(np.asarray(x, np.float32).astype(ml_dtypes.bfloat16).astype(np.float64), axis, -1)
    blocks = v.reshape(v.shape[:-1] + (-1, 32))
    amax = np.abs(blocks).max(-1, keepdims=True)
    byte = np.maximum(np.where(amax > 0, np.frexp(amax)[1] - 1 + 127, 0) - down, 1)
    scale = np.exp2(byte - 127.0)
    codes = (blocks / scale).astype(np.float32).astype(dtype).astype(np.float64)
    return np.moveaxis((codes * scale).reshape(v.shape), -1, axis)


WIDE = False


def mx_kscale(k):
    if not WIDE:
        return np.ones(k)
    levels = np.array([10, -10, 5, -5, 0])
    if k % 512:
        return np.exp2(np.random.permutation(np.resize(levels, k // 32))).repeat(32)
    a = np.empty((k // 512, 16))
    for p in range(k // 512):
        a[p, :8] = np.random.permutation(np.resize(levels, 8))
        for g in range(8):
            far = levels[np.abs(levels - a[p, g]) >= 10]
            a[p, g + 8] = far[np.random.randint(len(far))]
    return np.exp2(a.ravel()).repeat(32)


def f64(x):
    return np.asarray(x).astype(np.float64)


def striped(idx):
    return np.tile(np.asarray(idx).reshape(-1, 16).T, (8, 1)).astype(np.uint16)


def unstriped(offs):
    return offs[:16].T.reshape(-1).astype(np.int64)


E2M1 = np.array([0.0, 0.5, 1.0, 1.5, 2.0, 3.0, 4.0, 6.0, -0.0, -0.5, -1.0, -1.5, -2.0, -3.0, -4.0, -6.0])


def pack_weight(w, fmt):
    k, n = w.shape
    w = f64(np.asarray(w, np.float32).astype(ml_dtypes.bfloat16)).reshape(k // 32, 32, n)
    amax = np.abs(w).max(1)
    if fmt == "e4m3":
        byte = np.frexp(amax)[1] - 1 + 127 - 7
    else:
        mant, ex = np.frexp(amax / 6.0)
        byte = np.where(mant > 0.5, ex, ex - 1) + 127
    byte = np.clip(np.where(amax > 0, byte, 1), 1, 254)
    scaled = (w * np.exp2(127.0 - byte)[:, None, :]).reshape(k, n).astype(np.float32)
    by_word = np.ascontiguousarray(scaled.reshape(k // 512, 128, 4, n).transpose(0, 1, 3, 2))
    if fmt == "e4m3":
        words = by_word.astype(ml_dtypes.float8_e4m3fn).view(np.uint8)
    else:
        c = by_word.astype(ml_dtypes.float4_e2m1fn).view(np.uint8) & 0xF
        words = (c[..., 0::2] | (c[..., 1::2] << 4)).reshape(k // 512, 128, 2 * n)
    return np.ascontiguousarray(words), np.ascontiguousarray(byte.astype(np.uint8).reshape(k // 512, 16, n))


def unpack_weight(words, scales, fmt):
    g, _, n = scales.shape
    words = np.ascontiguousarray(words).reshape(g, 128, n, -1)
    if fmt == "e4m3":
        vals = words.view(ml_dtypes.float8_e4m3fn).astype(np.float64)
    else:
        nib = np.empty((g, 128, n, 4), np.uint8)
        nib[..., 0::2] = words & 0xF
        nib[..., 1::2] = words >> 4
        vals = E2M1[nib]
    vals = vals * np.repeat(np.exp2(scales.astype(np.float64) - 127.0), 8, axis=1)[..., None]
    return vals.transpose(0, 1, 3, 2).reshape(g * 512, n)


K, T, J, I, N = 1024, 1024, 512, 512, 512


def setup_inputs():
    n = np.random.standard_normal
    idx = np.random.permutation(T)[:J]
    idx2 = np.random.permutation(T)[:I]
    fk = mx_kscale(K)
    xqp = pack_weight(n((K, T)) / fk[:, None], "e4m3")
    return {
        "xq_words": xqp[0],
        "xq_scales": xqp[1],
        "wa": (n((K, N)) * 1 / np.sqrt(K) * fk[:, None]).astype(np.float32),
        "xr": (1.0 * n((N, T))).astype(np.float32),
        "gb": (np.random.uniform(0.5, 2.0, (1, I))).astype(np.float32),
        "ko": (np.random.uniform(-0.5, 0.5, (N, 1))).astype(np.float32),
        "offs": striped(idx),
        "offs2": striped(idx2),
    }


def reference(xq_words, xq_scales, wa, xr, gb, ko, offs, offs2):
    idx = unstriped(offs)
    idx2 = unstriped(offs2)
    xqu = unpack_weight(xq_words, xq_scales, "e4m3")
    waq = mxq(f64(wa), 0, "e4m3")
    xqidxg = xqu[:, idx]
    p = waq.T @ xqidxg
    pg = np.zeros((N, T))
    pg[:, idx] = p
    d = f64(xr)[:, idx2] * f64(gb) + f64(ko)
    dp = np.zeros((N, T))
    dp[:, idx2] = d
    y = pg + 0.5 * dp
    return y

@@ -1,0 +1,220 @@
+from contextlib import ExitStack
+
+import concourse.mybir as mybir
+from concourse.masks import make_identity
+
+K, T, J, I, N = 1024, 1024, 512, 512, 512
+FLOPS = 2 * K * N * J
+
+F32 = mybir.dt.float32
+BF16 = mybir.dt.bfloat16
+I32 = mybir.dt.int32
+U32 = mybir.dt.uint32
+U16 = mybir.dt.uint16
+U8 = mybir.dt.uint8
+FP8X4 = mybir.dt.float8_e4m3fn_x4
+MULT = mybir.AluOpType.mult
+ADD = mybir.AluOpType.add
+COPY = mybir.ActivationFunctionType.Copy
+IDENTITY = mybir.ActivationFunctionType.Identity
+
+P = 128
+PACK = 4
+K_PASS = P * PACK
+PASSES = K // K_PASS
+ROW_TILES = N // P
+W_HALF = N // 2
+LIST_COLS = J // 16
+HALF_COLS = LIST_COLS // 2
+HALF = J // 2
+
+
+def tile_list_copying_expert_kernel(tc, xq_words, xq_scales, wa, xr, gb, ko, offs, offs2, out):
+    nc = tc.nc
+    with ExitStack() as ctx:
+        pool = ctx.enter_context(tc.tile_pool(name="sb", bufs=1))
+        ps = ctx.enter_context(tc.psum_pool(name="ps", bufs=1))
+
+        def tile(shape, dtype, name, after=None):
+            return pool.tile(shape, dtype, name=name, tag=after or name, align_bytes=64)
+
+        list1 = pool.tile([P, LIST_COLS], U16, name="list1")
+        list2 = pool.tile([P, LIST_COLS], U16, name="list2")
+        gb_dealt = tile([P, 4], F32, "gb_dealt")
+        ko_rows = tile([P, P], F32, "ko_rows")
+        ko_half = tile([P, ROW_TILES], F32, "ko_half")
+        gb_rows = tile([P, I], F32, "gb_rows")
+        ident = tile([P, P], F32, "ident")
+        xr_t = [tile([P, T], F32, "xr%d" % c) for c in range(ROW_TILES)]
+        xw = [tile([P, T], I32, "xw%d" % z) for z in range(PASSES)]
+        xs = tile([P, T], U8, "xs")
+        w_raw = {(h, z): tile([P, PACK, W_HALF], F32, "w_raw%d%d" % (h, z)) for h in range(2) for z in range(PASSES)}
+        p_page = [tile([P, T], F32, "p_page%d" % b) for b in range(3)]
+        d_page = [tile([P, T], F32, "d_page%d" % b) for b in range(3)]
+
+        def load_xr(c):
+            nc.sync.dma_start(out=xr_t[c][:], in_=xr[c * P : (c + 1) * P, :])
+
+        def load_w(h, z):
+            rows = wa[z * K_PASS : (z + 1) * K_PASS, h * W_HALF : (h + 1) * W_HALF]
+            nc.sync.dma_start(out=w_raw[h, z][:], in_=rows.rearrange("(p j) n -> p j n", j=PACK))
+
+        nc.vector.memset(xs[:].bitcast(I32), 0)
+        nc.gpsimd.memset(ko_rows[:], 0.0)
+        make_identity(nc, ident[:])
+
+        nc.sync.dma_start(out=gb_dealt[:], in_=gb.rearrange("o (p c) -> (o p) c", c=4))
+        nc.sync.dma_start(list2[:], offs2)
+        load_xr(0)
+        nc.sync.dma_start(out=ko_rows[0:ROW_TILES, :], in_=ko.rearrange("(c p) o -> c (p o)", p=P))
+        load_xr(1)
+        nc.sync.dma_start(list1[:], offs)
+        for z in range(PASSES):
+            nc.sync.dma_start(out=xw[z][:], in_=xq_words[z].rearrange("p n t -> p (n t)").bitcast(I32))
+        for q in range(4):
+            nc.sync.dma_start(
+                out=xs[32 * q : 32 * q + 4 * PASSES, :].bitcast(I32),
+                in_=xq_scales[:, 4 * q : 4 * q + 4, :].bitcast(I32),
+            )
+        for h in range(2):
+            for z in range(PASSES):
+                load_w(h, z)
+        load_xr(2)
+        load_xr(3)
+
+        gb_bank = ps.tile([P, 4, P], F32, name="gb_bank")
+        for c in range(4):
+            nc.tensor.transpose(gb_bank[:, c, :], gb_dealt[:, c : c + 1].to_broadcast([P, P]), ident[:])
+        nc.scalar.copy(
+            out=gb_rows[:].rearrange("m (p c) -> m p c", c=4),
+            in_=gb_bank[:].rearrange("m c p -> m p c"),
+        )
+        ko_bank = ps.tile([P, P], F32, name="ko_bank")
+        nc.tensor.transpose(ko_bank[:], ko_rows[:], ident[:])
+        nc.scalar.activation(out=ko_half[:], in_=ko_bank[:, 0:ROW_TILES], func=COPY, scale=0.5)
+
+        for b in range(3):
+            nc.vector.memset(d_page[b][:], 0.0)
+            nc.vector.memset(p_page[b][:], 0.0)
+        p_page.append(tile([P, T], F32, "p_page3", after="ko_rows"))
+        d_page.append(tile([P, T], F32, "d_page3", after="ident"))
+        nc.gpsimd.memset(p_page[3][:], 0.0)
+        nc.gpsimd.memset(d_page[3][:], 0.0)
+
+        def list_half(lst, u):
+            return lst[:, u * HALF_COLS : (u + 1) * HALF_COLS]
+
+        def scatter_scalar(page, lst, vals):
+            for u in range(2):
+                nc.scalar.activation(
+                    out=page[:].indirect(list_half(lst, u)), in_=vals[:, u * HALF : (u + 1) * HALF], func=COPY
+                )
+
+        def scatter_vector(page, lst, vals):
+            nc.vector.tensor_copy(out=page[:].indirect(lst[:]), in_=vals[:])
+
+        prod0 = tile([P, I], F32, "prod0")
+        d_half0 = tile([P, I], F32, "d_half0")
+        for u in range(2):
+            cols = slice(u * HALF, (u + 1) * HALF)
+            nc.vector.tensor_tensor(prod0[:, cols], xr_t[0][:].indirect(list_half(list2, u)), gb_rows[:, cols], MULT)
+            nc.scalar.activation(
+                out=d_half0[:, cols], in_=prod0[:, cols], func=IDENTITY, scale=0.5, bias=ko_half[:, 0:1]
+            )
+            nc.scalar.activation(out=d_page[0][:].indirect(list_half(list2, u)), in_=d_half0[:, cols], func=COPY)
+
+        prod1 = tile([P, I], F32, "prod1")
+        d_half1 = tile([P, I], F32, "d_half1")
+        nc.vector.tensor_tensor(prod1[:], xr_t[1][:].indirect(list2[:]), gb_rows[:], MULT)
+        nc.gpsimd.tensor_scalar(d_half1[:], prod1[:], 0.5, ko_half[:, 1:2], MULT, ADD)
+        scatter_scalar(d_page[1], list2, d_half1)
+
+        xg = [tile([P, J], U32, "xg%d" % z, after="xr%d" % (1 - z)) for z in range(PASSES)]
+        xsg = tile([P, J], U8, "xsg", after="prod0")
+        for z in range(PASSES):
+            nc.vector.tensor_copy(out=xg[z][:], in_=xw[z][:].bitcast(U32).indirect(list1[:]))
+        nc.vector.tensor_copy(out=xsg[:], in_=xs[:].indirect(list1[:]))
+
+        w_codes = {}
+        w_scales = {}
+        slots = {(0, 0): "prod1", (0, 1): "xw0", (1, 0): "xw1", (1, 1): "xs"}
+        for h in range(2):
+            for z in range(PASSES):
+                grouped = tile([P, W_HALF, PACK], BF16, "w_bf%d%d" % (h, z), after=slots[h, z])
+                if (h, z) == (0, 0):
+                    nc.gpsimd.tensor_scalar(
+                        grouped[:], w_raw[h, z][:].rearrange("p j n -> p n j"), 1.0, 0.0, MULT, ADD
+                    )
+                else:
+                    nc.vector.tensor_copy(
+                        out=grouped[:].rearrange("p (c i) j -> p c j i", i=4),
+                        in_=w_raw[h, z][:].rearrange("p j (c i) -> p c j i", i=4),
+                    )
+                w_codes[h, z] = tile([P, W_HALF], U32, "w_codes%d%d" % (h, z))
+                w_scales[h, z] = tile([P, W_HALF], U8, "w_scales%d%d" % (h, z))
+                nc.vector.quantize_mx(
+                    out=w_codes[h, z][:].bitcast(FP8X4),
+                    scales=w_scales[h, z][:],
+                    in_=grouped[:].rearrange("p n j -> p (n j)"),
+                )
+
+        banks = []
+        for c in range(ROW_TILES):
+            bank = ps.tile([P, J], F32, name="p_bank%d" % c)
+            h, m = divmod(c, 2)
+            for z in range(PASSES):
+                nc.tensor.matmul_mx(
+                    out=bank[:],
+                    lhsT=w_codes[h, z][:, m * P : (m + 1) * P].bitcast(FP8X4),
+                    lhsT_scale=w_scales[h, z][:, m * P : (m + 1) * P],
+                    rhs=xg[z][:].bitcast(FP8X4),
+                    rhs_scale=xsg[4 * z : P, :],
+                    start=(z == 0),
+                    stop=(z == PASSES - 1),
+                )
+            banks.append(bank)
+
+        def add_and_store(c, after):
+            res = tile([P, T], F32, "res%d" % c, after=after)
+            nc.gpsimd.tensor_tensor(res[:], p_page[c][:], d_page[c][:], ADD)
+            nc.sync.dma_start(out=out[c * P : (c + 1) * P, :], in_=res[:])
+
+        for u in range(2):
+            p_sb0 = tile([P, HALF], F32, "p_sb0%d" % u)
+            nc.scalar.copy(out=p_sb0[:], in_=banks[0][:, u * HALF : (u + 1) * HALF])
+            nc.scalar.activation(out=p_page[0][:].indirect(list_half(list1, u)), in_=p_sb0[:], func=COPY)
+
+        prod2 = tile([P, I], F32, "prod2", after="xs")
+        d_half2 = tile([P, I], F32, "d_half2")
+        nc.vector.tensor_tensor(prod2[:], xr_t[2][:].indirect(list2[:]), gb_rows[:], MULT)
+        p_sb1 = tile([P, J], F32, "p_sb1", after="xr2")
+        nc.vector.tensor_copy(out=p_sb1[:], in_=banks[1][:])
+        nc.vector.tensor_scalar(d_half2[:], prod2[:], 0.5, ko_half[:, 2:3], MULT, ADD)
+        scatter_vector(p_page[1], list1, p_sb1)
+        scatter_vector(d_page[2], list2, d_half2)
+
+        add_and_store(0, None)
+
+        picked3 = tile([P, I], F32, "picked3", after="p_sb01")
+        prod3 = tile([P, I], F32, "prod3", after="p_page0")
+        d_half3 = tile([P, I], F32, "d_half3", after="xr2")
+        nc.scalar.activation(out=picked3[:], in_=xr_t[3][:].indirect(list2[:]), func=COPY)
+        nc.gpsimd.tensor_tensor(prod3[:], picked3[:], gb_rows[:], MULT)
+        nc.gpsimd.tensor_scalar(d_half3[:], prod3[:], 0.5, ko_half[:, 3:4], MULT, ADD)
+
+        add_and_store(1, "p_page0")
+
+        p_sb2 = tile([P, J], F32, "p_sb2", after="xr3")
+        nc.scalar.copy(out=p_sb2[:], in_=banks[2][:])
+        scatter_scalar(p_page[2], list1, p_sb2)
+        add_and_store(2, "p_page1")
+
+        p_sb3 = tile([P, J], F32, "p_sb3", after="xr3")
+        nc.scalar.copy(out=p_sb3[:], in_=banks[3][:])
+        scatter_scalar(p_page[3], list1, p_sb3)
+        scatter_vector(d_page[3], list2, d_half3)
+        res3 = tile([P, T], F32, "res3")
+        for u, queue in enumerate((nc.sync, nc.scalar)):
+            cols = slice(u * T // 2, (u + 1) * T // 2)
+            nc.vector.tensor_tensor(res3[:, cols], p_page[3][:, cols], d_page[3][:, cols], ADD)
+            queue.dma_start(out=out[3 * P : 4 * P, cols], in_=res3[:, cols])

@@ -27,6 +27,7 @@ W_HALF = N // 2
 LIST_COLS = J // 16
 HALF_COLS = LIST_COLS // 2
 HALF = J // 2
+FIRST = 128
 
 
 def tile_list_copying_expert_kernel(tc, xq_words, xq_scales, wa, xr, gb, ko, offs, offs2, out):
@@ -63,11 +64,12 @@ def tile_list_copying_expert_kernel(tc, xq_words, xq_scales, wa, xr, gb, ko, off
         nc.gpsimd.memset(ko_rows[:], 0.0)
         make_identity(nc, ident[:])
 
-        nc.sync.dma_start(out=gb_dealt[:], in_=gb.rearrange("o (p c) -> (o p) c", c=4))
+        nc.scalar.dma_start(out=gb_dealt[:], in_=gb.rearrange("o (p c) -> (o p) c", c=4))
         nc.sync.dma_start(list2[:], offs2)
         load_xr(0)
-        nc.sync.dma_start(out=ko_rows[0:ROW_TILES, :], in_=ko.rearrange("(c p) o -> c (p o)", p=P))
+        nc.scalar.dma_start(out=ko_rows[0:ROW_TILES, :], in_=ko.rearrange("(c p) o -> c (p o)", p=P))
         load_xr(1)
+        load_xr(2)
         nc.sync.dma_start(list1[:], offs)
         for z in range(PASSES):
             nc.sync.dma_start(out=xw[z][:], in_=xq_words[z].rearrange("p n t -> p (n t)").bitcast(I32))
@@ -79,57 +81,60 @@ def tile_list_copying_expert_kernel(tc, xq_words, xq_scales, wa, xr, gb, ko, off
         for h in range(2):
             for z in range(PASSES):
                 load_w(h, z)
-        load_xr(2)
         load_xr(3)
+
+        for page in d_page[:2]:
+            nc.vector.memset(page[:].bitcast(I32), 0)
+        for page in d_page[2:] + p_page:
+            nc.gpsimd.memset(page[:].bitcast(I32), 0)
 
         gb_bank = ps.tile([P, 4, P], F32, name="gb_bank")
         for c in range(4):
             nc.tensor.transpose(gb_bank[:, c, :], gb_dealt[:, c : c + 1].to_broadcast([P, P]), ident[:])
-        nc.scalar.copy(
-            out=gb_rows[:].rearrange("m (p c) -> m p c", c=4),
-            in_=gb_bank[:].rearrange("m c p -> m p c"),
-        )
+        pieces = (slice(0, FIRST), slice(FIRST, I))
+        for cols in pieces:
+            nc.scalar.copy(
+                out=gb_rows[:, cols].rearrange("m (p c) -> m p c", c=4),
+                in_=gb_bank[:, :, cols.start // 4 : cols.stop // 4].rearrange("m c p -> m p c"),
+            )
         ko_bank = ps.tile([P, P], F32, name="ko_bank")
         nc.tensor.transpose(ko_bank[:], ko_rows[:], ident[:])
         nc.scalar.activation(out=ko_half[:], in_=ko_bank[:, 0:ROW_TILES], func=COPY, scale=0.5)
 
-        for b in range(3):
-            nc.vector.memset(d_page[b][:], 0.0)
-            nc.vector.memset(p_page[b][:], 0.0)
-        p_page.append(tile([P, T], F32, "p_page3", after="ko_rows"))
-        d_page.append(tile([P, T], F32, "d_page3", after="ident"))
-        nc.gpsimd.memset(p_page[3][:], 0.0)
-        nc.gpsimd.memset(d_page[3][:], 0.0)
+        def entries(lst, cols):
+            return lst[:, cols.start // 16 : cols.stop // 16]
 
-        def list_half(lst, u):
-            return lst[:, u * HALF_COLS : (u + 1) * HALF_COLS]
+        halves = (slice(0, HALF), slice(HALF, J))
 
         def scatter_scalar(page, lst, vals):
-            for u in range(2):
-                nc.scalar.activation(
-                    out=page[:].indirect(list_half(lst, u)), in_=vals[:, u * HALF : (u + 1) * HALF], func=COPY
-                )
-
-        def scatter_vector(page, lst, vals):
-            nc.vector.tensor_copy(out=page[:].indirect(lst[:]), in_=vals[:])
+            for cols in halves:
+                nc.scalar.activation(out=page[:].indirect(entries(lst, cols)), in_=vals[:, cols], func=COPY)
 
         prod0 = tile([P, I], F32, "prod0")
-        d_half0 = tile([P, I], F32, "d_half0")
-        for u in range(2):
-            cols = slice(u * HALF, (u + 1) * HALF)
-            nc.vector.tensor_tensor(prod0[:, cols], xr_t[0][:].indirect(list_half(list2, u)), gb_rows[:, cols], MULT)
-            nc.scalar.activation(
-                out=d_half0[:, cols], in_=prod0[:, cols], func=IDENTITY, scale=0.5, bias=ko_half[:, 0:1]
-            )
-            nc.scalar.activation(out=d_page[0][:].indirect(list_half(list2, u)), in_=d_half0[:, cols], func=COPY)
+        d0 = tile([P, I], F32, "d0")
+        for cols in pieces:
+            nc.vector.tensor_tensor(prod0[:, cols], xr_t[0][:].indirect(entries(list2, cols)), gb_rows[:, cols], MULT)
+            nc.scalar.activation(out=d0[:, cols], in_=prod0[:, cols], func=IDENTITY, scale=0.5, bias=ko_half[:, 0:1])
+            nc.scalar.activation(out=d_page[0][:].indirect(entries(list2, cols)), in_=d0[:, cols], func=COPY)
 
-        prod1 = tile([P, I], F32, "prod1")
-        d_half1 = tile([P, I], F32, "d_half1")
-        nc.vector.tensor_tensor(prod1[:], xr_t[1][:].indirect(list2[:]), gb_rows[:], MULT)
-        nc.gpsimd.tensor_scalar(d_half1[:], prod1[:], 0.5, ko_half[:, 1:2], MULT, ADD)
-        scatter_scalar(d_page[1], list2, d_half1)
+        def pick_and_scale(c, after=None):
+            prod = tile([P, I], F32, "prod%d" % c, after=after)
+            nc.vector.tensor_tensor(prod[:], xr_t[c][:].indirect(list2[:]), gb_rows[:], MULT)
+            return prod
 
-        xg = [tile([P, J], U32, "xg%d" % z, after="xr%d" % (1 - z)) for z in range(PASSES)]
+        def finish_d(c, prod, name, after=None):
+            half_d = tile(list(prod.shape), F32, name, after=after)
+            nc.gpsimd.tensor_scalar(half_d[:], prod, 0.5, ko_half[:, c : c + 1], MULT, ADD)
+            return half_d
+
+        prod1 = pick_and_scale(1)
+        d1 = finish_d(1, prod1[:], "d1")
+        prod2 = pick_and_scale(2)
+        d2a = finish_d(2, prod2[:, halves[0]], "d2a")
+        scatter_scalar(d_page[1], list2, d1)
+        nc.scalar.activation(out=d_page[2][:].indirect(entries(list2, halves[0])), in_=d2a[:], func=COPY)
+
+        xg = [tile([P, J], U32, "xg%d" % z, after="xr%d" % (2 - z)) for z in range(PASSES)]
         xsg = tile([P, J], U8, "xsg", after="prod0")
         for z in range(PASSES):
             nc.vector.tensor_copy(out=xg[z][:], in_=xw[z][:].bitcast(U32).indirect(list1[:]))
@@ -137,36 +142,36 @@ def tile_list_copying_expert_kernel(tc, xq_words, xq_scales, wa, xr, gb, ko, off
 
         w_codes = {}
         w_scales = {}
-        slots = {(0, 0): "prod1", (0, 1): "xw0", (1, 0): "xw1", (1, 1): "xs"}
-        for h in range(2):
+
+        def quantise_w(h, cols, name):
+            width = cols.stop - cols.start
+            grouped = []
             for z in range(PASSES):
-                grouped = tile([P, W_HALF, PACK], BF16, "w_bf%d%d" % (h, z), after=slots[h, z])
-                if (h, z) == (0, 0):
-                    nc.gpsimd.tensor_scalar(
-                        grouped[:], w_raw[h, z][:].rearrange("p j n -> p n j"), 1.0, 0.0, MULT, ADD
-                    )
-                else:
-                    nc.vector.tensor_copy(
-                        out=grouped[:].rearrange("p (c i) j -> p c j i", i=4),
-                        in_=w_raw[h, z][:].rearrange("p j (c i) -> p c j i", i=4),
-                    )
-                w_codes[h, z] = tile([P, W_HALF], U32, "w_codes%d%d" % (h, z))
-                w_scales[h, z] = tile([P, W_HALF], U8, "w_scales%d%d" % (h, z))
+                grouped.append(tile([P, width, PACK], BF16, "w_bf%s%d" % (name, z), after="xw%d" % z))
+                nc.vector.tensor_copy(out=grouped[z][:], in_=w_raw[h, z][:, :, cols].rearrange("p j n -> p n j"))
+            for z in range(PASSES):
+                codes = tile([P, width], U32, "w_codes%s%d" % (name, z))
+                scales = tile([P, width], U8, "w_scales%s%d" % (name, z))
                 nc.vector.quantize_mx(
-                    out=w_codes[h, z][:].bitcast(FP8X4),
-                    scales=w_scales[h, z][:],
-                    in_=grouped[:].rearrange("p n j -> p (n j)"),
+                    out=codes[:].bitcast(FP8X4), scales=scales[:], in_=grouped[z][:].rearrange("p n j -> p (n j)")
                 )
+                for m in range(width // P):
+                    c = (h * W_HALF + cols.start) // P + m
+                    w_codes[c, z] = codes[:, m * P : (m + 1) * P]
+                    w_scales[c, z] = scales[:, m * P : (m + 1) * P]
+
+        quantise_w(0, slice(0, P), "a")
+        quantise_w(0, slice(P, W_HALF), "b")
+        quantise_w(1, slice(0, W_HALF), "c")
 
         banks = []
         for c in range(ROW_TILES):
             bank = ps.tile([P, J], F32, name="p_bank%d" % c)
-            h, m = divmod(c, 2)
             for z in range(PASSES):
                 nc.tensor.matmul_mx(
                     out=bank[:],
-                    lhsT=w_codes[h, z][:, m * P : (m + 1) * P].bitcast(FP8X4),
-                    lhsT_scale=w_scales[h, z][:, m * P : (m + 1) * P],
+                    lhsT=w_codes[c, z].bitcast(FP8X4),
+                    lhsT_scale=w_scales[c, z],
                     rhs=xg[z][:].bitcast(FP8X4),
                     rhs_scale=xsg[4 * z : P, :],
                     start=(z == 0),
@@ -174,47 +179,36 @@ def tile_list_copying_expert_kernel(tc, xq_words, xq_scales, wa, xr, gb, ko, off
                 )
             banks.append(bank)
 
-        def add_and_store(c, after):
+        def add_and_store(c, pp, dp, after=None):
             res = tile([P, T], F32, "res%d" % c, after=after)
-            nc.gpsimd.tensor_tensor(res[:], p_page[c][:], d_page[c][:], ADD)
+            nc.gpsimd.tensor_tensor(res[:], pp[:], dp[:], ADD)
             nc.sync.dma_start(out=out[c * P : (c + 1) * P, :], in_=res[:])
 
-        for u in range(2):
-            p_sb0 = tile([P, HALF], F32, "p_sb0%d" % u)
-            nc.scalar.copy(out=p_sb0[:], in_=banks[0][:, u * HALF : (u + 1) * HALF])
-            nc.scalar.activation(out=p_page[0][:].indirect(list_half(list1, u)), in_=p_sb0[:], func=COPY)
+        p_sb0 = tile([P, J], F32, "p_sb0")
+        for cols in halves:
+            nc.scalar.copy(out=p_sb0[:, cols], in_=banks[0][:, cols])
+        scatter_scalar(p_page[0], list1, p_sb0)
 
-        prod2 = tile([P, I], F32, "prod2", after="xs")
-        d_half2 = tile([P, I], F32, "d_half2")
-        nc.vector.tensor_tensor(prod2[:], xr_t[2][:].indirect(list2[:]), gb_rows[:], MULT)
-        p_sb1 = tile([P, J], F32, "p_sb1", after="xr2")
+        prod3 = pick_and_scale(3, after="xw0")
+        d3 = finish_d(3, prod3[:], "d3")
+        d2b = finish_d(2, prod2[:, halves[1]], "d2b", after="xr3")
+        p_sb1 = tile([P, J], F32, "p_sb1", after="gb_rows")
         nc.vector.tensor_copy(out=p_sb1[:], in_=banks[1][:])
-        nc.vector.tensor_scalar(d_half2[:], prod2[:], 0.5, ko_half[:, 2:3], MULT, ADD)
-        scatter_vector(p_page[1], list1, p_sb1)
-        scatter_vector(d_page[2], list2, d_half2)
+        nc.vector.tensor_copy(out=p_page[1][:].indirect(list1[:]), in_=p_sb1[:])
+        nc.vector.tensor_copy(out=d_page[2][:].indirect(entries(list2, halves[1])), in_=d2b[:])
+        add_and_store(0, p_page[0], d_page[0], after="xw0")
+        add_and_store(1, p_page[1], d_page[1])
 
-        add_and_store(0, None)
-
-        picked3 = tile([P, I], F32, "picked3", after="p_sb01")
-        prod3 = tile([P, I], F32, "prod3", after="p_page0")
-        d_half3 = tile([P, I], F32, "d_half3", after="xr2")
-        nc.scalar.activation(out=picked3[:], in_=xr_t[3][:].indirect(list2[:]), func=COPY)
-        nc.gpsimd.tensor_tensor(prod3[:], picked3[:], gb_rows[:], MULT)
-        nc.gpsimd.tensor_scalar(d_half3[:], prod3[:], 0.5, ko_half[:, 3:4], MULT, ADD)
-
-        add_and_store(1, "p_page0")
-
-        p_sb2 = tile([P, J], F32, "p_sb2", after="xr3")
+        p_sb2 = tile([P, J], F32, "p_sb2", after="d1")
         nc.scalar.copy(out=p_sb2[:], in_=banks[2][:])
         scatter_scalar(p_page[2], list1, p_sb2)
-        add_and_store(2, "p_page1")
+        add_and_store(2, p_page[2], d_page[2])
 
-        p_sb3 = tile([P, J], F32, "p_sb3", after="xr3")
+        p_sb3 = tile([P, J], F32, "p_sb3", after="p_sb0")
         nc.scalar.copy(out=p_sb3[:], in_=banks[3][:])
-        scatter_scalar(p_page[3], list1, p_sb3)
-        scatter_vector(d_page[3], list2, d_half3)
+        scatter_scalar(p_page[0], list1, p_sb3)
+        nc.vector.tensor_copy(out=d_page[0][:].indirect(list2[:]), in_=d3[:])
         res3 = tile([P, T], F32, "res3")
-        for u, queue in enumerate((nc.sync, nc.scalar)):
-            cols = slice(u * T // 2, (u + 1) * T // 2)
-            nc.vector.tensor_tensor(res3[:, cols], p_page[3][:, cols], d_page[3][:, cols], ADD)
+        for cols, queue in ((slice(0, 512), nc.sync), (slice(512, 768), nc.scalar), (slice(768, T), nc.sync)):
+            nc.vector.tensor_tensor(res3[:, cols], p_page[0][:, cols], d_page[0][:, cols], ADD)
             queue.dma_start(out=out[3 * P : 4 * P, cols], in_=res3[:, cols])

from contextlib import ExitStack

import concourse.mybir as mybir
from concourse.masks import make_identity

K, T, J, I, N = 1024, 1024, 512, 512, 512
FLOPS = 2 * K * N * J

F32 = mybir.dt.float32
BF16 = mybir.dt.bfloat16
I32 = mybir.dt.int32
U32 = mybir.dt.uint32
U16 = mybir.dt.uint16
U8 = mybir.dt.uint8
FP8X4 = mybir.dt.float8_e4m3fn_x4
MULT = mybir.AluOpType.mult
ADD = mybir.AluOpType.add
COPY = mybir.ActivationFunctionType.Copy
IDENTITY = mybir.ActivationFunctionType.Identity

P = 128
PACK = 4
K_PASS = P * PACK
PASSES = K // K_PASS
ROW_TILES = N // P
W_HALF = N // 2
LIST_COLS = J // 16
HALF_COLS = LIST_COLS // 2
HALF = J // 2
FIRST = 128


def tile_list_copying_expert_kernel(tc, xq_words, xq_scales, wa, xr, gb, ko, offs, offs2, out):
    nc = tc.nc
    with ExitStack() as ctx:
        pool = ctx.enter_context(tc.tile_pool(name="sb", bufs=1))
        ps = ctx.enter_context(tc.psum_pool(name="ps", bufs=1))

        def tile(shape, dtype, name, after=None):
            return pool.tile(shape, dtype, name=name, tag=after or name, align_bytes=64)

        list1 = pool.tile([P, LIST_COLS], U16, name="list1")
        list2 = pool.tile([P, LIST_COLS], U16, name="list2")
        gb_dealt = tile([P, 4], F32, "gb_dealt")
        ko_rows = tile([P, P], F32, "ko_rows")
        ko_half = tile([P, ROW_TILES], F32, "ko_half")
        gb_rows = tile([P, I], F32, "gb_rows")
        ident = tile([P, P], F32, "ident")
        xr_t = [tile([P, T], F32, "xr%d" % c) for c in range(ROW_TILES)]
        xw = [tile([P, T], I32, "xw%d" % z) for z in range(PASSES)]
        xs = tile([P, T], U8, "xs")
        w_raw = {(h, z): tile([P, PACK, W_HALF], F32, "w_raw%d%d" % (h, z)) for h in range(2) for z in range(PASSES)}
        p_page = [tile([P, T], F32, "p_page%d" % b) for b in range(3)]
        d_page = [tile([P, T], F32, "d_page%d" % b) for b in range(3)]

        def load_xr(c):
            nc.sync.dma_start(out=xr_t[c][:], in_=xr[c * P : (c + 1) * P, :])

        def load_w(h, z):
            rows = wa[z * K_PASS : (z + 1) * K_PASS, h * W_HALF : (h + 1) * W_HALF]
            nc.sync.dma_start(out=w_raw[h, z][:], in_=rows.rearrange("(p j) n -> p j n", j=PACK))

        nc.vector.memset(xs[:].bitcast(I32), 0)
        nc.gpsimd.memset(ko_rows[:], 0.0)
        make_identity(nc, ident[:])

        nc.scalar.dma_start(out=gb_dealt[:], in_=gb.rearrange("o (p c) -> (o p) c", c=4))
        nc.sync.dma_start(list2[:], offs2)
        load_xr(0)
        nc.scalar.dma_start(out=ko_rows[0:ROW_TILES, :], in_=ko.rearrange("(c p) o -> c (p o)", p=P))
        load_xr(1)
        load_xr(2)
        nc.sync.dma_start(list1[:], offs)
        for z in range(PASSES):
            nc.sync.dma_start(out=xw[z][:], in_=xq_words[z].rearrange("p n t -> p (n t)").bitcast(I32))
        for q in range(4):
            nc.sync.dma_start(
                out=xs[32 * q : 32 * q + 4 * PASSES, :].bitcast(I32),
                in_=xq_scales[:, 4 * q : 4 * q + 4, :].bitcast(I32),
            )
        for h in range(2):
            for z in range(PASSES):
                load_w(h, z)
        load_xr(3)

        for page in d_page[:2]:
            nc.vector.memset(page[:].bitcast(I32), 0)
        for page in d_page[2:] + p_page:
            nc.gpsimd.memset(page[:].bitcast(I32), 0)

        gb_bank = ps.tile([P, 4, P], F32, name="gb_bank")
        for c in range(4):
            nc.tensor.transpose(gb_bank[:, c, :], gb_dealt[:, c : c + 1].to_broadcast([P, P]), ident[:])
        pieces = (slice(0, FIRST), slice(FIRST, I))
        for cols in pieces:
            nc.scalar.copy(
                out=gb_rows[:, cols].rearrange("m (p c) -> m p c", c=4),
                in_=gb_bank[:, :, cols.start // 4 : cols.stop // 4].rearrange("m c p -> m p c"),
            )
        ko_bank = ps.tile([P, P], F32, name="ko_bank")
        nc.tensor.transpose(ko_bank[:], ko_rows[:], ident[:])
        nc.scalar.activation(out=ko_half[:], in_=ko_bank[:, 0:ROW_TILES], func=COPY, scale=0.5)

        def entries(lst, cols):
            return lst[:, cols.start // 16 : cols.stop // 16]

        halves = (slice(0, HALF), slice(HALF, J))

        def scatter_scalar(page, lst, vals):
            for cols in halves:
                nc.scalar.activation(out=page[:].indirect(entries(lst, cols)), in_=vals[:, cols], func=COPY)

        prod0 = tile([P, I], F32, "prod0")
        d0 = tile([P, I], F32, "d0")
        for cols in pieces:
            nc.vector.tensor_tensor(prod0[:, cols], xr_t[0][:].indirect(entries(list2, cols)), gb_rows[:, cols], MULT)
            nc.scalar.activation(out=d0[:, cols], in_=prod0[:, cols], func=IDENTITY, scale=0.5, bias=ko_half[:, 0:1])
            nc.scalar.activation(out=d_page[0][:].indirect(entries(list2, cols)), in_=d0[:, cols], func=COPY)

        def pick_and_scale(c, after=None):
            prod = tile([P, I], F32, "prod%d" % c, after=after)
            nc.vector.tensor_tensor(prod[:], xr_t[c][:].indirect(list2[:]), gb_rows[:], MULT)
            return prod

        def finish_d(c, prod, name, after=None):
            half_d = tile(list(prod.shape), F32, name, after=after)
            nc.gpsimd.tensor_scalar(half_d[:], prod, 0.5, ko_half[:, c : c + 1], MULT, ADD)
            return half_d

        prod1 = pick_and_scale(1)
        d1 = finish_d(1, prod1[:], "d1")
        prod2 = pick_and_scale(2)
        d2a = finish_d(2, prod2[:, halves[0]], "d2a")
        scatter_scalar(d_page[1], list2, d1)
        nc.scalar.activation(out=d_page[2][:].indirect(entries(list2, halves[0])), in_=d2a[:], func=COPY)

        xg = [tile([P, J], U32, "xg%d" % z, after="xr%d" % (2 - z)) for z in range(PASSES)]
        xsg = tile([P, J], U8, "xsg", after="prod0")
        for z in range(PASSES):
            nc.vector.tensor_copy(out=xg[z][:], in_=xw[z][:].bitcast(U32).indirect(list1[:]))
        nc.vector.tensor_copy(out=xsg[:], in_=xs[:].indirect(list1[:]))

        w_codes = {}
        w_scales = {}

        def quantise_w(h, cols, name):
            width = cols.stop - cols.start
            grouped = []
            for z in range(PASSES):
                grouped.append(tile([P, width, PACK], BF16, "w_bf%s%d" % (name, z), after="xw%d" % z))
                nc.vector.tensor_copy(out=grouped[z][:], in_=w_raw[h, z][:, :, cols].rearrange("p j n -> p n j"))
            for z in range(PASSES):
                codes = tile([P, width], U32, "w_codes%s%d" % (name, z))
                scales = tile([P, width], U8, "w_scales%s%d" % (name, z))
                nc.vector.quantize_mx(
                    out=codes[:].bitcast(FP8X4), scales=scales[:], in_=grouped[z][:].rearrange("p n j -> p (n j)")
                )
                for m in range(width // P):
                    c = (h * W_HALF + cols.start) // P + m
                    w_codes[c, z] = codes[:, m * P : (m + 1) * P]
                    w_scales[c, z] = scales[:, m * P : (m + 1) * P]

        quantise_w(0, slice(0, P), "a")
        quantise_w(0, slice(P, W_HALF), "b")
        quantise_w(1, slice(0, W_HALF), "c")

        banks = []
        for c in range(ROW_TILES):
            bank = ps.tile([P, J], F32, name="p_bank%d" % c)
            for z in range(PASSES):
                nc.tensor.matmul_mx(
                    out=bank[:],
                    lhsT=w_codes[c, z].bitcast(FP8X4),
                    lhsT_scale=w_scales[c, z],
                    rhs=xg[z][:].bitcast(FP8X4),
                    rhs_scale=xsg[4 * z : P, :],
                    start=(z == 0),
                    stop=(z == PASSES - 1),
                )
            banks.append(bank)

        def add_and_store(c, pp, dp, after=None):
            res = tile([P, T], F32, "res%d" % c, after=after)
            nc.gpsimd.tensor_tensor(res[:], pp[:], dp[:], ADD)
            nc.sync.dma_start(out=out[c * P : (c + 1) * P, :], in_=res[:])

        p_sb0 = tile([P, J], F32, "p_sb0")
        for cols in halves:
            nc.scalar.copy(out=p_sb0[:, cols], in_=banks[0][:, cols])
        scatter_scalar(p_page[0], list1, p_sb0)

        prod3 = pick_and_scale(3, after="xw0")
        d3 = finish_d(3, prod3[:], "d3")
        d2b = finish_d(2, prod2[:, halves[1]], "d2b", after="xr3")
        p_sb1 = tile([P, J], F32, "p_sb1", after="gb_rows")
        nc.vector.tensor_copy(out=p_sb1[:], in_=banks[1][:])
        nc.vector.tensor_copy(out=p_page[1][:].indirect(list1[:]), in_=p_sb1[:])
        nc.vector.tensor_copy(out=d_page[2][:].indirect(entries(list2, halves[1])), in_=d2b[:])
        add_and_store(0, p_page[0], d_page[0], after="xw0")
        add_and_store(1, p_page[1], d_page[1])

        p_sb2 = tile([P, J], F32, "p_sb2", after="d1")
        nc.scalar.copy(out=p_sb2[:], in_=banks[2][:])
        scatter_scalar(p_page[2], list1, p_sb2)
        add_and_store(2, p_page[2], d_page[2])

        p_sb3 = tile([P, J], F32, "p_sb3", after="p_sb0")
        nc.scalar.copy(out=p_sb3[:], in_=banks[3][:])
        scatter_scalar(p_page[0], list1, p_sb3)
        nc.vector.tensor_copy(out=d_page[0][:].indirect(list2[:]), in_=d3[:])
        res3 = tile([P, T], F32, "res3")
        for cols, queue in ((slice(0, 512), nc.sync), (slice(512, 768), nc.scalar), (slice(768, T), nc.sync)):
            nc.vector.tensor_tensor(res3[:, cols], p_page[0][:, cols], d_page[0][:, cols], ADD)
            queue.dma_start(out=out[3 * P : 4 * P, cols], in_=res3[:, cols])
